import numpy as np
import ml_dtypes


def mxq(x, axis, fmt="e4m3"):
    dtype, down = {"e4m3": (ml_dtypes.float8_e4m3fn, 7), "e5m2": (ml_dtypes.float8_e5m2, 14)}[fmt]
    v = np.moveaxis(np.asarray(x, np.float32).astype(ml_dtypes.bfloat16).astype(np.float64), axis, -1)
    blocks = v.reshape(v.shape[:-1] + (-1, 32))
    amax = np.abs(blocks).max(-1, keepdims=True)
    byte = np.maximum(np.where(amax > 0, np.frexp(amax)[1] - 1 + 127, 0) - down, 1)
    scale = np.exp2(byte - 127.0)
    codes = (blocks / scale).astype(np.float32).astype(dtype).astype(np.float64)
    return np.moveaxis((codes * scale).reshape(v.shape), -1, axis)


WIDE = False


def mx_kscale(k):
    if not WIDE:
        return np.ones(k)
    levels = np.array([30, -30])
    if k % 512:
        return np.exp2(np.random.permutation(np.resize(levels, k // 32))).repeat(32)
    a = np.empty((k // 512, 16))
    for p in range(k // 512):
        a[p, :8] = np.random.permutation(np.resize(levels, 8))
        for g in range(8):
            far = levels[np.abs(levels - a[p, g]) >= 10]
            a[p, g + 8] = far[np.random.randint(len(far))]
    return np.exp2(a.ravel()).repeat(32)


def f64(x):
    return np.asarray(x).astype(np.float64)


def striped(idx):
    return np.tile(np.asarray(idx).reshape(-1, 16).T, (8, 1)).astype(np.uint16)


def unstriped(offs):
    return offs[:16].T.reshape(-1).astype(np.int64)


def striped8(idx):
    return np.asarray(idx).reshape(8, -1, 16).transpose(0, 2, 1).reshape(128, -1).astype(np.uint16)


def unstriped8(offs):
    return offs.reshape(8, 16, -1).transpose(0, 2, 1).reshape(8, -1).astype(np.int64)


def pick8(x, idx, run):
    r = np.arange(len(x))
    return x[r[:, None], idx[r % (8 * run) // run]]


E2M1 = np.array([0.0, 0.5, 1.0, 1.5, 2.0, 3.0, 4.0, 6.0, -0.0, -0.5, -1.0, -1.5, -2.0, -3.0, -4.0, -6.0])


def pack_weight(w, fmt):
    k, n = w.shape
    w = f64(np.asarray(w, np.float32).astype(ml_dtypes.bfloat16)).reshape(k // 32, 32, n)
    amax = np.abs(w).max(1)
    if fmt in ("e4m3", "e5m2"):
        byte = np.frexp(amax)[1] - 1 + 127 - (7 if fmt == "e4m3" else 14)
    else:
        mant, ex = np.frexp(amax / 6.0)
        byte = np.where(mant > 0.5, ex, ex - 1) + 127
    byte = np.clip(np.where(amax > 0, byte, 1), 1, 254)
    scaled = (w * np.exp2(127.0 - byte)[:, None, :]).reshape(k, n).astype(np.float32)
    by_word = np.ascontiguousarray(scaled.reshape(k // 512, 128, 4, n).transpose(0, 1, 3, 2))
    if fmt in ("e4m3", "e5m2"):
        words = by_word.astype(ml_dtypes.float8_e4m3fn if fmt == "e4m3" else ml_dtypes.float8_e5m2).view(np.uint8)
    else:
        c = by_word.astype(ml_dtypes.float4_e2m1fn).view(np.uint8) & 0xF
        words = (c[..., 0::2] | (c[..., 1::2] << 4)).reshape(k // 512, 128, 2 * n)
    return np.ascontiguousarray(words), np.ascontiguousarray(byte.astype(np.uint8).reshape(k // 512, 16, n))


def unpack_weight(words, scales, fmt):
    g, _, n = scales.shape
    words = np.ascontiguousarray(words).reshape(g, 128, n, -1)
    if fmt in ("e4m3", "e5m2"):
        vals = words.view(ml_dtypes.float8_e4m3fn if fmt == "e4m3" else ml_dtypes.float8_e5m2).astype(np.float64)
    else:
        nib = np.empty((g, 128, n, 4), np.uint8)
        nib[..., 0::2] = words & 0xF
        nib[..., 1::2] = words >> 4
        vals = E2M1[nib]
    vals = vals * np.repeat(np.exp2(scales.astype(np.float64) - 127.0), 8, axis=1)[..., None]
    return vals.transpose(0, 1, 3, 2).reshape(g * 512, n)


def bf(x):
    return np.asarray(x, np.float32).astype(ml_dtypes.bfloat16)


def planes(Y):
    r, m = Y.shape
    b = f64(bf(Y)).reshape(r // 32, 32, m)
    amax = np.abs(b).max(1)
    byte = np.clip(np.where(amax > 0, np.frexp(amax)[1] - 1 + 127 - 7, 1), 1, 254)
    codes = (b * np.exp2(127.0 - byte)[:, None, :]).reshape(r, m).astype(np.float32).astype(ml_dtypes.float8_e4m3fn).view(np.uint8)
    words = codes.reshape(r // 512, 128, 4, m).transpose(0, 1, 3, 2)
    return np.ascontiguousarray(words), np.ascontiguousarray(byte.astype(np.uint8).reshape(r // 512, 16, m))


K, T, J, R, G, N, Z = 1024, 512, 256, 512, 32, 512, 512


def setup_inputs():
    n = np.random.standard_normal
    idx = np.stack([np.random.permutation(T)[:J] for _ in range(8)])
    idx2 = np.random.permutation(Z)[:J]
    fk = mx_kscale(K)
    fr = mx_kscale(R)
    xtp = pack_weight(n((K, T)) / fk[:, None], "e4m3")
    wp = pack_weight(n((K, R)) * 1 / np.sqrt(K) * fk[:, None] * fr, "e2m1")
    wbp = pack_weight(n((R, N)) * 1 / np.sqrt(R) / fr[:, None], "e5m2")
    return {
        "xt_words": xtp[0],
        "xt_scales": xtp[1],
        "w_words": wp[0],
        "w_scales": wp[1],
        "wb_words": wbp[0],
        "wb_scales": wbp[1],
        "tz": (n((N, Z))).astype(np.float32),
        "offs": striped8(idx),
        "offs2": striped(idx2),
    }


def reference(xt_words, xt_scales, w_words, w_scales, wb_words, wb_scales, tz, offs, offs2):
    idx = unstriped8(offs)
    idx2 = unstriped(offs2)
    xtu = unpack_weight(xt_words, xt_scales, "e4m3")
    wu = unpack_weight(w_words, w_scales, "e2m1")
    wbu = unpack_weight(wb_words, wb_scales, "e5m2")
    xtidxg = pick8(xtu, idx, 64)
    a = wu.T @ xtidxg
    m1 = a.reshape(R, G, J // G).mean(axis=2)
    m2 = np.repeat(m1, J // G, axis=1)
    hid = a - m2
    hidq = mxq(hid, 0, "e5m2")
    p = wbu.T @ hidq
    y = p * f64(tz)[:, idx2]
    words, scales = planes(y)
    return y, words, scales

@@ -1,0 +1,177 @@
+from contextlib import ExitStack
+
+import concourse.mybir as mybir
+
+K, T, J, R, N, Z = 1024, 512, 256, 512, 512, 512
+FLOPS = 2 * K * R * J + 2 * R * N * J
+
+F32 = mybir.dt.float32
+BF16 = mybir.dt.bfloat16
+I32 = mybir.dt.int32
+U32 = mybir.dt.uint32
+U16 = mybir.dt.uint16
+U8 = mybir.dt.uint8
+E4M3 = mybir.dt.float8_e4m3fn_x4
+E5M2 = mybir.dt.float8_e5m2_x4
+E2M1 = mybir.dt.float4_e2m1fn_x4
+ALU = mybir.AluOpType
+COPY = mybir.ActivationFunctionType.Copy
+
+P = 128
+PACK = 4
+PASSES = K // (P * PACK)
+HALF = 128
+HALVES = J // HALF
+BUNDLE = 8
+GH = HALF // BUNDLE
+
+
+def tile_list_headpicks_levelled_timeslook_pl_kernel(
+    tc, xt_words, xt_scales, w_words, w_scales, wb_words, wb_scales, tz, offs, offs2, out_0, out_1, out_2
+):
+    nc = tc.nc
+    with ExitStack() as ctx:
+        keep = ctx.enter_context(tc.tile_pool(name="keep", bufs=1))
+        psum = ctx.enter_context(tc.psum_pool(name="psum", bufs=1))
+
+        lists = keep.tile([P, J // 16], U16, name="lists")
+        lists2 = keep.tile([P, J // 16], U16, name="lists2")
+        xs_win = keep.tile([P, T], U8, name="xs_win", align_bytes=64)
+        ws_raw = keep.tile([P, R], U8, name="ws_raw", tag="late", align_bytes=64)
+        wbs_raw = keep.tile([P, N], U8, name="wbs_raw", align_bytes=64)
+        plane = keep.tile([P, PASSES, J + R], U8, name="plane", align_bytes=64)
+
+        nc.vector.memset(xs_win[:].bitcast(I32), 0)
+        nc.vector.memset(ws_raw[:].bitcast(I32), 0)
+        nc.gpsimd.memset(wbs_raw[:].bitcast(I32), 0)
+        nc.gpsimd.memset(plane[:].rearrange("p z c -> p (z c)").bitcast(I32), 0)
+
+        nc.sync.dma_start(lists[:], offs)
+        nc.scalar.dma_start(xs_win[0:P:4, :].bitcast(I32), xt_scales.bitcast(I32).rearrange("z q c -> q z c"))
+        nc.scalar.dma_start(ws_raw[0:P:4, :].bitcast(I32), w_scales.bitcast(I32).rearrange("z q c -> q z c"))
+
+        xw_win = [keep.tile([P, T], I32, name="xw_win%d" % z, align_bytes=64) for z in range(PASSES)]
+        for z in range(PASSES):
+            nc.sync.dma_start(xw_win[z][:], xt_words[z].rearrange("p c r -> p (c r)").bitcast(I32))
+        ww_raw = keep.tile([P, PASSES, R // 2], I32, name="ww_raw", align_bytes=64)
+        nc.sync.dma_start(ww_raw[:], w_words.bitcast(I32).rearrange("z p c -> p z c"))
+        nc.sync.dma_start(lists2[:], offs2)
+        wbw_raw = keep.tile([P, N], I32, name="wbw_raw", align_bytes=64)
+        nc.sync.dma_start(wbw_raw[:], wb_words[0].rearrange("p c r -> p (c r)").bitcast(I32))
+
+        xs_got = keep.tile([P, J], U8, name="xs_got", align_bytes=64)
+        nc.vector.tensor_copy(xs_got[:], xs_win[:].indirect(lists[:]))
+        staged = keep.tile([P, J + R], U8, name="staged", align_bytes=64)
+        nc.vector.tensor_copy(
+            staged[:, J:].rearrange("p (t c i) -> p c t i", t=PACK, i=16),
+            ws_raw[:].rearrange("p (c i t) -> p c t i", t=PACK, i=16),
+        )
+        nc.vector.tensor_copy(staged[:, :J].bitcast(I32), xs_got[:].bitcast(I32))
+        for x in range(4):
+            eng = nc.sync if x % 2 == 0 else nc.scalar
+            eng.dma_start(
+                plane[32 * x : 32 * x + 4].rearrange("p z c -> p (z c)").bitcast(I32),
+                staged[32 * x : 32 * x + 32 : 4, :].bitcast(I32),
+            )
+
+        tz_win = keep.tile([P, PACK, Z], F32, name="tz_win", tag="late", align_bytes=64)
+        tz_rows = tz.rearrange("(p t) z -> p t z", t=PACK)
+        for t in range(PACK):
+            nc.sync.dma_start(tz_win[:, t, :], tz_rows[:, t, :])
+        for x in range(4):
+            nc.sync.dma_start(
+                wbs_raw[32 * x : 32 * x + 4, :].bitcast(I32), wb_scales[0, 4 * x : 4 * x + 4, :].bitcast(I32)
+            )
+
+        xw_got = keep.tile([P, PASSES, J], U32, name="xw_got", align_bytes=64)
+        for z in range(PASSES):
+            nc.vector.tensor_copy(xw_got[:, z, :], xw_win[z][:].bitcast(U32).indirect(lists[:]))
+        ww = keep.tile([P, PASSES, 2 * R], U8, name="ww", align_bytes=64)
+        for z in range(PASSES):
+            nc.vector.tensor_copy(
+                ww[:, z, :].bitcast(U16).rearrange("p (t c i) -> p c t i", t=PACK, i=8),
+                ww_raw[:, z, :].bitcast(U16).rearrange("p (c i t) -> p c t i", t=PACK, i=8),
+            )
+
+        a_ps = [psum.tile([P, PACK, HALF], F32, name="a_ps%d" % h) for h in range(HALVES)]
+        for h in range(HALVES):
+            cols = slice(h * HALF, (h + 1) * HALF)
+            for t in range(PACK):
+                for z in range(PASSES):
+                    nc.tensor.matmul_mx(
+                        out=a_ps[h][:, t, :],
+                        lhsT=ww[:, z, 2 * P * t : 2 * P * (t + 1)].bitcast(E2M1),
+                        lhsT_scale=plane[:, z, J + P * t : J + P * (t + 1)],
+                        rhs=xw_got[:, z, cols].bitcast(E4M3),
+                        rhs_scale=plane[:, z, cols],
+                        start=(z == 0),
+                        stop=(z == PASSES - 1),
+                    )
+
+        wbw = keep.tile([P, N], I32, name="wbw", align_bytes=64)
+        nc.vector.tensor_copy(
+            wbw[:].rearrange("p (t c i) -> p c t i", t=PACK, i=4),
+            wbw_raw[:].rearrange("p (c i t) -> p c t i", t=PACK, i=4),
+        )
+        wbs = keep.tile([P, N], U8, name="wbs", align_bytes=64)
+        nc.vector.tensor_copy(
+            wbs[:].rearrange("p (t c i) -> p c t i", t=PACK, i=16),
+            wbs_raw[:].rearrange("p (c i t) -> p c t i", t=PACK, i=16),
+        )
+
+        tz_got = keep.tile([P, PACK, J], F32, name="tz_got", align_bytes=64)
+        for t in range(PACK):
+            nc.scalar.activation(tz_got[:, t, :], tz_win[:, t, :].indirect(lists2[:]), COPY)
+
+        out_rows = out_0.rearrange("(p t) j -> p t j", t=PACK)
+        y_words = keep.tile([P, J], I32, name="y_words", align_bytes=64)
+        y_scales = keep.tile([P, J], U8, name="y_scales", align_bytes=64)
+        p_ps = [psum.tile([P, PACK, HALF], F32, name="p_ps%d" % h) for h in range(HALVES)]
+        for h in range(HALVES):
+            sums = keep.tile([P, GH, PACK], F32, name="sums%d" % h, align_bytes=64)
+            by_bundle = a_ps[h][:].rearrange("p t (g e) -> p g t e", e=BUNDLE)
+            nc.vector.tensor_reduce(sums[:], by_bundle, mybir.AxisListType.X, ALU.add)
+            hid = keep.tile([P, BUNDLE, GH, PACK], BF16, name="hid%d" % h, align_bytes=64)
+            for e in range(BUNDLE):
+                nc.vector.scalar_tensor_tensor(
+                    hid[:, e], sums[:], -1.0 / BUNDLE, by_bundle[:, :, :, e], ALU.mult, ALU.add
+                )
+            hid_words = keep.tile([P, HALF], U32, name="hid_words%d" % h, align_bytes=64)
+            hid_scales = keep.tile([P, HALF], U8, name="hid_scales%d" % h, align_bytes=64)
+            nc.vector.quantize_mx(
+                out=hid_words[:].bitcast(E5M2), scales=hid_scales[:], in_=hid[:].rearrange("p e g t -> p (e g t)")
+            )
+            for t in range(PACK):
+                nc.tensor.matmul_mx(
+                    out=p_ps[h][:, t, :],
+                    lhsT=wbw[:, P * t : P * (t + 1)].bitcast(E5M2),
+                    lhsT_scale=wbs[:, P * t : P * (t + 1)],
+                    rhs=hid_words[:].bitcast(E5M2),
+                    rhs_scale=hid_scales[:],
+                    start=True,
+                    stop=True,
+                )
+        for h in range(HALVES):
+            cols = slice(h * HALF, (h + 1) * HALF)
+            y = keep.tile([P, PACK, HALF], F32, name="y%d" % h, align_bytes=64)
+            nc.vector.tensor_tensor(
+                y[:].rearrange("p t (g e) -> p t g e", e=BUNDLE),
+                p_ps[h][:].rearrange("p t (e g) -> p t g e", e=BUNDLE),
+                tz_got[:, :, cols].rearrange("p t (g e) -> p t g e", e=BUNDLE),
+                ALU.mult,
+            )
+            nc.sync.dma_start(out_rows[:, :, cols], y[:])
+            y_bf = keep.tile([P, HALF, PACK], BF16, name="y_bf%d" % h, align_bytes=64)
+            dst = y_bf[:].rearrange("p (c i) t -> p c t i", i=4)
+            src = y[:].rearrange("p t (c i) -> p c t i", i=4)
+            if h == 0:
+                nc.scalar.copy(dst, src)
+            else:
+                nc.vector.tensor_copy(dst, src)
+            nc.vector.quantize_mx(
+                out=y_words[:, cols].bitcast(E4M3), scales=y_scales[:, cols], in_=y_bf[:].rearrange("p j t -> p (j t)")
+            )
+        nc.scalar.dma_start(out_1[0].rearrange("p c r -> p (c r)").bitcast(I32), y_words[:])
+        for x in range(4):
+            eng = nc.sync if x % 2 == 0 else nc.scalar
+            eng.dma_start(out_2[0, 4 * x : 4 * x + 4, :].bitcast(I32), y_scales[32 * x : 32 * x + 4, :].bitcast(I32))

@@ -36,30 +36,28 @@ def tile_list_headpicks_levelled_timeslook_pl_kernel(
 
         lists = keep.tile([P, J // 16], U16, name="lists")
         lists2 = keep.tile([P, J // 16], U16, name="lists2")
-        xs_win = keep.tile([P, T], U8, name="xs_win", align_bytes=64)
-        ws_raw = keep.tile([P, R], U8, name="ws_raw", tag="late", align_bytes=64)
-        wbs_raw = keep.tile([P, N], U8, name="wbs_raw", align_bytes=64)
+        xs_win = keep.tile([P, T], U8, name="xs_win", tag="xs_win", align_bytes=64)
+        ws_raw = keep.tile([P, R], U8, name="ws_raw", tag="ws_raw", align_bytes=64)
         plane = keep.tile([P, PASSES, J + R], U8, name="plane", align_bytes=64)
 
         nc.vector.memset(xs_win[:].bitcast(I32), 0)
         nc.vector.memset(ws_raw[:].bitcast(I32), 0)
-        nc.gpsimd.memset(wbs_raw[:].bitcast(I32), 0)
         nc.gpsimd.memset(plane[:].rearrange("p z c -> p (z c)").bitcast(I32), 0)
 
         nc.sync.dma_start(lists[:], offs)
         nc.scalar.dma_start(xs_win[0:P:4, :].bitcast(I32), xt_scales.bitcast(I32).rearrange("z q c -> q z c"))
         nc.scalar.dma_start(ws_raw[0:P:4, :].bitcast(I32), w_scales.bitcast(I32).rearrange("z q c -> q z c"))
 
-        xw_win = [keep.tile([P, T], I32, name="xw_win%d" % z, align_bytes=64) for z in range(PASSES)]
+        xw_win = [keep.tile([P, T], I32, name="xw_win%d" % z, tag="xw_win%d" % z, align_bytes=64) for z in range(PASSES)]
         for z in range(PASSES):
             nc.sync.dma_start(xw_win[z][:], xt_words[z].rearrange("p c r -> p (c r)").bitcast(I32))
         ww_raw = keep.tile([P, PASSES, R // 2], I32, name="ww_raw", align_bytes=64)
         nc.sync.dma_start(ww_raw[:], w_words.bitcast(I32).rearrange("z p c -> p z c"))
         nc.sync.dma_start(lists2[:], offs2)
-        wbw_raw = keep.tile([P, N], I32, name="wbw_raw", align_bytes=64)
-        nc.sync.dma_start(wbw_raw[:], wb_words[0].rearrange("p c r -> p (c r)").bitcast(I32))
+        tz_win = keep.tile([P, PACK, Z], F32, name="tz_win", align_bytes=64)
+        nc.sync.dma_start(tz_win[:], tz.rearrange("(p t) z -> p t z", t=PACK))
 
-        xs_got = keep.tile([P, J], U8, name="xs_got", align_bytes=64)
+        xs_got = keep.tile([P, J], U8, name="xs_got", tag="xs_got", align_bytes=64)
         nc.vector.tensor_copy(xs_got[:], xs_win[:].indirect(lists[:]))
         staged = keep.tile([P, J + R], U8, name="staged", align_bytes=64)
         nc.vector.tensor_copy(
@@ -68,25 +66,26 @@ def tile_list_headpicks_levelled_timeslook_pl_kernel(
         )
         nc.vector.tensor_copy(staged[:, :J].bitcast(I32), xs_got[:].bitcast(I32))
         for x in range(4):
-            eng = nc.sync if x % 2 == 0 else nc.scalar
-            eng.dma_start(
+            nc.scalar.dma_start(
                 plane[32 * x : 32 * x + 4].rearrange("p z c -> p (z c)").bitcast(I32),
                 staged[32 * x : 32 * x + 32 : 4, :].bitcast(I32),
             )
 
-        tz_win = keep.tile([P, PACK, Z], F32, name="tz_win", tag="late", align_bytes=64)
-        tz_rows = tz.rearrange("(p t) z -> p t z", t=PACK)
-        for t in range(PACK):
-            nc.sync.dma_start(tz_win[:, t, :], tz_rows[:, t, :])
+        xw_got = [
+            keep.tile([P, J], U32, name="xw_got%d" % z, tag=("ws_raw", "xs_got")[z], align_bytes=64)
+            for z in range(PASSES)
+        ]
+        for z in range(PASSES):
+            nc.vector.tensor_copy(xw_got[z][:], xw_win[z][:].bitcast(U32).indirect(lists[:]))
+        wbw_raw = keep.tile([P, N], I32, name="wbw_raw", tag="xw_win0", align_bytes=64)
+        nc.sync.dma_start(wbw_raw[:], wb_words[0].rearrange("p c r -> p (c r)").bitcast(I32))
+        wbs_raw = keep.tile([P, N], U8, name="wbs_raw", tag="xw_win1", align_bytes=64)
+        nc.gpsimd.memset(wbs_raw[:].bitcast(I32), 0)
         for x in range(4):
             nc.sync.dma_start(
                 wbs_raw[32 * x : 32 * x + 4, :].bitcast(I32), wb_scales[0, 4 * x : 4 * x + 4, :].bitcast(I32)
             )
-
-        xw_got = keep.tile([P, PASSES, J], U32, name="xw_got", align_bytes=64)
-        for z in range(PASSES):
-            nc.vector.tensor_copy(xw_got[:, z, :], xw_win[z][:].bitcast(U32).indirect(lists[:]))
-        ww = keep.tile([P, PASSES, 2 * R], U8, name="ww", align_bytes=64)
+        ww = keep.tile([P, PASSES, 2 * R], U8, name="ww", tag="xs_win", align_bytes=64)
         for z in range(PASSES):
             nc.vector.tensor_copy(
                 ww[:, z, :].bitcast(U16).rearrange("p (t c i) -> p c t i", t=PACK, i=8),
@@ -102,7 +101,7 @@ def tile_list_headpicks_levelled_timeslook_pl_kernel(
                         out=a_ps[h][:, t, :],
                         lhsT=ww[:, z, 2 * P * t : 2 * P * (t + 1)].bitcast(E2M1),
                         lhsT_scale=plane[:, z, J + P * t : J + P * (t + 1)],
-                        rhs=xw_got[:, z, cols].bitcast(E4M3),
+                        rhs=xw_got[z][:, cols].bitcast(E4M3),
                         rhs_scale=plane[:, z, cols],
                         start=(z == 0),
                         stop=(z == PASSES - 1),
@@ -124,14 +123,15 @@ def tile_list_headpicks_levelled_timeslook_pl_kernel(
             nc.scalar.activation(tz_got[:, t, :], tz_win[:, t, :].indirect(lists2[:]), COPY)
 
         out_rows = out_0.rearrange("(p t) j -> p t j", t=PACK)
+        out_words = out_1[0].rearrange("p c r -> p (c r)").bitcast(I32)
         y_words = keep.tile([P, J], I32, name="y_words", align_bytes=64)
         y_scales = keep.tile([P, J], U8, name="y_scales", align_bytes=64)
         p_ps = [psum.tile([P, PACK, HALF], F32, name="p_ps%d" % h) for h in range(HALVES)]
         for h in range(HALVES):
-            sums = keep.tile([P, GH, PACK], F32, name="sums%d" % h, align_bytes=64)
+            sums = keep.tile([P, GH, PACK], F32, name="sums%d" % h, tag="sums", align_bytes=64)
             by_bundle = a_ps[h][:].rearrange("p t (g e) -> p g t e", e=BUNDLE)
             nc.vector.tensor_reduce(sums[:], by_bundle, mybir.AxisListType.X, ALU.add)
-            hid = keep.tile([P, BUNDLE, GH, PACK], BF16, name="hid%d" % h, align_bytes=64)
+            hid = keep.tile([P, BUNDLE, GH, PACK], BF16, name="hid%d" % h, tag="hid", align_bytes=64)
             for e in range(BUNDLE):
                 nc.vector.scalar_tensor_tensor(
                     hid[:, e], sums[:], -1.0 / BUNDLE, by_bundle[:, :, :, e], ALU.mult, ALU.add
@@ -153,7 +153,7 @@ def tile_list_headpicks_levelled_timeslook_pl_kernel(
                 )
         for h in range(HALVES):
             cols = slice(h * HALF, (h + 1) * HALF)
-            y = keep.tile([P, PACK, HALF], F32, name="y%d" % h, align_bytes=64)
+            y = keep.tile([P, PACK, HALF], F32, name="y%d" % h, tag=("hid", "y1")[h], align_bytes=64)
             nc.vector.tensor_tensor(
                 y[:].rearrange("p t (g e) -> p t g e", e=BUNDLE),
                 p_ps[h][:].rearrange("p t (e g) -> p t g e", e=BUNDLE),
@@ -171,7 +171,7 @@ def tile_list_headpicks_levelled_timeslook_pl_kernel(
             nc.vector.quantize_mx(
                 out=y_words[:, cols].bitcast(E4M3), scales=y_scales[:, cols], in_=y_bf[:].rearrange("p j t -> p (j t)")
             )
-        nc.scalar.dma_start(out_1[0].rearrange("p c r -> p (c r)").bitcast(I32), y_words[:])
+            nc.sync.dma_start(out_words[:, cols], y_words[:, cols])
         for x in range(4):
-            eng = nc.sync if x % 2 == 0 else nc.scalar
+            eng = nc.scalar if x % 2 == 0 else nc.sync
             eng.dma_start(out_2[0, 4 * x : 4 * x + 4, :].bitcast(I32), y_scales[32 * x : 32 * x + 4, :].bitcast(I32))

@@ -23,6 +23,7 @@ PASSES = K // (P * PACK)
 HALF = 128
 HALVES = J // HALF
 BUNDLE = 8
+SLOTS = 4
 GH = HALF // BUNDLE
 
 
@@ -38,24 +39,26 @@ def tile_list_headpicks_levelled_timeslook_pl_kernel(
         lists2 = keep.tile([P, J // 16], U16, name="lists2")
         xs_win = keep.tile([P, T], U8, name="xs_win", tag="xs_win", align_bytes=64)
         ws_raw = keep.tile([P, R], U8, name="ws_raw", tag="ws_raw", align_bytes=64)
-        plane = keep.tile([P, PASSES, J + R], U8, name="plane", align_bytes=64)
-
+        plane = keep.tile([P, SLOTS, J + R], U8, name="plane", align_bytes=64)
         nc.vector.memset(xs_win[:].bitcast(I32), 0)
         nc.vector.memset(ws_raw[:].bitcast(I32), 0)
-        nc.gpsimd.memset(plane[:].rearrange("p z c -> p (z c)").bitcast(I32), 0)
+        nc.gpsimd.memset(plane[:].rearrange("p s c -> p (s c)").bitcast(I32), 0)
 
         nc.sync.dma_start(lists[:], offs)
-        nc.scalar.dma_start(xs_win[0:P:4, :].bitcast(I32), xt_scales.bitcast(I32).rearrange("z q c -> q z c"))
-        nc.scalar.dma_start(ws_raw[0:P:4, :].bitcast(I32), w_scales.bitcast(I32).rearrange("z q c -> q z c"))
-
-        xw_win = [keep.tile([P, T], I32, name="xw_win%d" % z, tag="xw_win%d" % z, align_bytes=64) for z in range(PASSES)]
+        nc.sync.dma_start(lists2[:], offs2)
+        nc.sync.dma_start(xs_win[0:P:4, :].bitcast(I32), xt_scales.bitcast(I32).rearrange("z q c -> q z c"))
+        nc.sync.dma_start(ws_raw[0:P:4, :].bitcast(I32), w_scales.bitcast(I32).rearrange("z q c -> q z c"))
+        nc.sync.dma_start(ws_raw[2:P:8, :].bitcast(I32), wb_scales[0].bitcast(I32))
+        xw_win = [keep.tile([P, T], I32, name="xw_win%d" % z, align_bytes=64) for z in range(PASSES)]
         for z in range(PASSES):
             nc.sync.dma_start(xw_win[z][:], xt_words[z].rearrange("p c r -> p (c r)").bitcast(I32))
-        ww_raw = keep.tile([P, PASSES, R // 2], I32, name="ww_raw", align_bytes=64)
+        ww_raw = keep.tile([P, PASSES, R // 2], I32, name="ww_raw", tag="ww_raw", align_bytes=64)
         nc.sync.dma_start(ww_raw[:], w_words.bitcast(I32).rearrange("z p c -> p z c"))
-        nc.sync.dma_start(lists2[:], offs2)
-        tz_win = keep.tile([P, PACK, Z], F32, name="tz_win", align_bytes=64)
-        nc.sync.dma_start(tz_win[:], tz.rearrange("(p t) z -> p t z", t=PACK))
+        wbw_raw = keep.tile([P, N], I32, name="wbw_raw", align_bytes=64)
+        nc.sync.dma_start(wbw_raw[:], wb_words[0].rearrange("p c r -> p (c r)").bitcast(I32))
+        tz_rows = tz.rearrange("(p t) z -> p t z", t=PACK)
+        tz_first = keep.tile([P, 1, Z], F32, name="tz_first", align_bytes=64)
+        nc.sync.dma_start(tz_first[:], tz_rows[:, 0:1, :])
 
         xs_got = keep.tile([P, J], U8, name="xs_got", tag="xs_got", align_bytes=64)
         nc.vector.tensor_copy(xs_got[:], xs_win[:].indirect(lists[:]))
@@ -66,31 +69,32 @@ def tile_list_headpicks_levelled_timeslook_pl_kernel(
         )
         nc.vector.tensor_copy(staged[:, :J].bitcast(I32), xs_got[:].bitcast(I32))
         for x in range(4):
-            nc.scalar.dma_start(
-                plane[32 * x : 32 * x + 4].rearrange("p z c -> p (z c)").bitcast(I32),
-                staged[32 * x : 32 * x + 32 : 4, :].bitcast(I32),
+            (nc.sync, nc.scalar)[x % 2].dma_start(
+                plane[32 * x : 32 * x + 4].rearrange("p s c -> p (s c)").bitcast(I32),
+                staged[32 * x : 32 * x + 32 : 2, :].bitcast(I32),
             )
+        tz_rest = keep.tile([P, PACK - 1, Z], F32, name="tz_rest", tag="xs_got", align_bytes=64)
+        nc.sync.dma_start(tz_rest[:, 0:1, :], tz_rows[:, 1:2, :])
+        nc.sync.dma_start(tz_rest[:, 1:3, :], tz_rows[:, 2:4, :])
+        tz_win = [tz_first[:, 0, :]] + [tz_rest[:, t, :] for t in range(PACK - 1)]
 
         xw_got = [
-            keep.tile([P, J], U32, name="xw_got%d" % z, tag=("ws_raw", "xs_got")[z], align_bytes=64)
+            keep.tile([P, J], U32, name="xw_got%d" % z, tag=("xs_win", "ws_raw")[z], align_bytes=64)
             for z in range(PASSES)
         ]
         for z in range(PASSES):
             nc.vector.tensor_copy(xw_got[z][:], xw_win[z][:].bitcast(U32).indirect(lists[:]))
-        wbw_raw = keep.tile([P, N], I32, name="wbw_raw", tag="xw_win0", align_bytes=64)
-        nc.sync.dma_start(wbw_raw[:], wb_words[0].rearrange("p c r -> p (c r)").bitcast(I32))
-        wbs_raw = keep.tile([P, N], U8, name="wbs_raw", tag="xw_win1", align_bytes=64)
-        nc.gpsimd.memset(wbs_raw[:].bitcast(I32), 0)
-        for x in range(4):
-            nc.sync.dma_start(
-                wbs_raw[32 * x : 32 * x + 4, :].bitcast(I32), wb_scales[0, 4 * x : 4 * x + 4, :].bitcast(I32)
-            )
-        ww = keep.tile([P, PASSES, 2 * R], U8, name="ww", tag="xs_win", align_bytes=64)
+        ww = keep.tile([P, PASSES, 2 * R], U8, name="ww", align_bytes=64)
         for z in range(PASSES):
             nc.vector.tensor_copy(
                 ww[:, z, :].bitcast(U16).rearrange("p (t c i) -> p c t i", t=PACK, i=8),
                 ww_raw[:, z, :].bitcast(U16).rearrange("p (c i t) -> p c t i", t=PACK, i=8),
             )
+        wbw = keep.tile([P, N], I32, name="wbw", tag="ww_raw", align_bytes=64)
+        nc.vector.tensor_copy(
+            wbw[:].rearrange("p (t c i) -> p c t i", t=PACK, i=4),
+            wbw_raw[:].rearrange("p (c i t) -> p c t i", t=PACK, i=4),
+        )
 
         a_ps = [psum.tile([P, PACK, HALF], F32, name="a_ps%d" % h) for h in range(HALVES)]
         for h in range(HALVES):
@@ -100,27 +104,16 @@ def tile_list_headpicks_levelled_timeslook_pl_kernel(
                     nc.tensor.matmul_mx(
                         out=a_ps[h][:, t, :],
                         lhsT=ww[:, z, 2 * P * t : 2 * P * (t + 1)].bitcast(E2M1),
-                        lhsT_scale=plane[:, z, J + P * t : J + P * (t + 1)],
+                        lhsT_scale=plane[:, 2 * z, J + P * t : J + P * (t + 1)],
                         rhs=xw_got[z][:, cols].bitcast(E4M3),
-                        rhs_scale=plane[:, z, cols],
+                        rhs_scale=plane[:, 2 * z, cols],
                         start=(z == 0),
                         stop=(z == PASSES - 1),
                     )
 
-        wbw = keep.tile([P, N], I32, name="wbw", align_bytes=64)
-        nc.vector.tensor_copy(
-            wbw[:].rearrange("p (t c i) -> p c t i", t=PACK, i=4),
-            wbw_raw[:].rearrange("p (c i t) -> p c t i", t=PACK, i=4),
-        )
-        wbs = keep.tile([P, N], U8, name="wbs", align_bytes=64)
-        nc.vector.tensor_copy(
-            wbs[:].rearrange("p (t c i) -> p c t i", t=PACK, i=16),
-            wbs_raw[:].rearrange("p (c i t) -> p c t i", t=PACK, i=16),
-        )
-
         tz_got = keep.tile([P, PACK, J], F32, name="tz_got", align_bytes=64)
         for t in range(PACK):
-            nc.scalar.activation(tz_got[:, t, :], tz_win[:, t, :].indirect(lists2[:]), COPY)
+            nc.scalar.activation(tz_got[:, t, :], tz_win[t].indirect(lists2[:]), COPY)
 
         out_rows = out_0.rearrange("(p t) j -> p t j", t=PACK)
         out_words = out_1[0].rearrange("p c r -> p (c r)").bitcast(I32)
@@ -145,7 +138,7 @@ def tile_list_headpicks_levelled_timeslook_pl_kernel(
                 nc.tensor.matmul_mx(
                     out=p_ps[h][:, t, :],
                     lhsT=wbw[:, P * t : P * (t + 1)].bitcast(E5M2),
-                    lhsT_scale=wbs[:, P * t : P * (t + 1)],
+                    lhsT_scale=plane[:, 1, J + P * t : J + P * (t + 1)],
                     rhs=hid_words[:].bitcast(E5M2),
                     rhs_scale=hid_scales[:],
                     start=True,

@@ -23,7 +23,6 @@ PASSES = K // (P * PACK)
 HALF = 128
 HALVES = J // HALF
 BUNDLE = 8
-SLOTS = 4
 GH = HALF // BUNDLE
 
 
@@ -39,10 +38,12 @@ def tile_list_headpicks_levelled_timeslook_pl_kernel(
         lists2 = keep.tile([P, J // 16], U16, name="lists2")
         xs_win = keep.tile([P, T], U8, name="xs_win", tag="xs_win", align_bytes=64)
         ws_raw = keep.tile([P, R], U8, name="ws_raw", tag="ws_raw", align_bytes=64)
-        plane = keep.tile([P, SLOTS, J + R], U8, name="plane", align_bytes=64)
+        plane = keep.tile([P, PASSES, J + R], U8, name="plane", align_bytes=64)
+        wbs = keep.tile([P, N], U8, name="wbs", align_bytes=64)
         nc.vector.memset(xs_win[:].bitcast(I32), 0)
         nc.vector.memset(ws_raw[:].bitcast(I32), 0)
         nc.gpsimd.memset(plane[:].rearrange("p s c -> p (s c)").bitcast(I32), 0)
+        nc.gpsimd.memset(wbs[:].bitcast(I32), 0)
 
         nc.sync.dma_start(lists[:], offs)
         nc.sync.dma_start(lists2[:], offs2)
@@ -71,11 +72,14 @@ def tile_list_headpicks_levelled_timeslook_pl_kernel(
         for x in range(4):
             (nc.sync, nc.scalar)[x % 2].dma_start(
                 plane[32 * x : 32 * x + 4].rearrange("p s c -> p (s c)").bitcast(I32),
-                staged[32 * x : 32 * x + 32 : 2, :].bitcast(I32),
+                staged[32 * x : 32 * x + 32 : 4, :].bitcast(I32),
             )
         tz_rest = keep.tile([P, PACK - 1, Z], F32, name="tz_rest", tag="xs_got", align_bytes=64)
-        nc.sync.dma_start(tz_rest[:, 0:1, :], tz_rows[:, 1:2, :])
-        nc.sync.dma_start(tz_rest[:, 1:3, :], tz_rows[:, 2:4, :])
+        nc.sync.dma_start(tz_rest[:], tz_rows[:, 1:PACK, :])
+        for x in range(4):
+            nc.sync.dma_start(
+                wbs[32 * x : 32 * x + 4, :].bitcast(I32), staged[32 * x + 2 : 32 * x + 32 : 8, J:].bitcast(I32)
+            )
         tz_win = [tz_first[:, 0, :]] + [tz_rest[:, t, :] for t in range(PACK - 1)]
 
         xw_got = [
@@ -104,9 +108,9 @@ def tile_list_headpicks_levelled_timeslook_pl_kernel(
                     nc.tensor.matmul_mx(
                         out=a_ps[h][:, t, :],
                         lhsT=ww[:, z, 2 * P * t : 2 * P * (t + 1)].bitcast(E2M1),
-                        lhsT_scale=plane[:, 2 * z, J + P * t : J + P * (t + 1)],
+                        lhsT_scale=plane[:, z, J + P * t : J + P * (t + 1)],
                         rhs=xw_got[z][:, cols].bitcast(E4M3),
-                        rhs_scale=plane[:, 2 * z, cols],
+                        rhs_scale=plane[:, z, cols],
                         start=(z == 0),
                         stop=(z == PASSES - 1),
                     )
@@ -124,7 +128,7 @@ def tile_list_headpicks_levelled_timeslook_pl_kernel(
             sums = keep.tile([P, GH, PACK], F32, name="sums%d" % h, tag="sums", align_bytes=64)
             by_bundle = a_ps[h][:].rearrange("p t (g e) -> p g t e", e=BUNDLE)
             nc.vector.tensor_reduce(sums[:], by_bundle, mybir.AxisListType.X, ALU.add)
-            hid = keep.tile([P, BUNDLE, GH, PACK], BF16, name="hid%d" % h, tag="hid", align_bytes=64)
+            hid = keep.tile([P, BUNDLE, GH, PACK], BF16, name="hid%d" % h, tag="hid%d" % h, align_bytes=64)
             for e in range(BUNDLE):
                 nc.vector.scalar_tensor_tensor(
                     hid[:, e], sums[:], -1.0 / BUNDLE, by_bundle[:, :, :, e], ALU.mult, ALU.add
@@ -138,7 +142,7 @@ def tile_list_headpicks_levelled_timeslook_pl_kernel(
                 nc.tensor.matmul_mx(
                     out=p_ps[h][:, t, :],
                     lhsT=wbw[:, P * t : P * (t + 1)].bitcast(E5M2),
-                    lhsT_scale=plane[:, 1, J + P * t : J + P * (t + 1)],
+                    lhsT_scale=wbs[:, P * t : P * (t + 1)],
                     rhs=hid_words[:].bitcast(E5M2),
                     rhs_scale=hid_scales[:],
                     start=True,
@@ -146,7 +150,7 @@ def tile_list_headpicks_levelled_timeslook_pl_kernel(
                 )
         for h in range(HALVES):
             cols = slice(h * HALF, (h + 1) * HALF)
-            y = keep.tile([P, PACK, HALF], F32, name="y%d" % h, tag=("hid", "y1")[h], align_bytes=64)
+            y = keep.tile([P, PACK, HALF], F32, name="y%d" % h, tag=("hid1", "y1")[h], align_bytes=64)
             nc.vector.tensor_tensor(
                 y[:].rearrange("p t (g e) -> p t g e", e=BUNDLE),
                 p_ps[h][:].rearrange("p t (e g) -> p t g e", e=BUNDLE),

from contextlib import ExitStack

import concourse.mybir as mybir

K, T, J, R, N, Z = 1024, 512, 256, 512, 512, 512
FLOPS = 2 * K * R * J + 2 * R * N * J

F32 = mybir.dt.float32
BF16 = mybir.dt.bfloat16
I32 = mybir.dt.int32
U32 = mybir.dt.uint32
U16 = mybir.dt.uint16
U8 = mybir.dt.uint8
E4M3 = mybir.dt.float8_e4m3fn_x4
E5M2 = mybir.dt.float8_e5m2_x4
E2M1 = mybir.dt.float4_e2m1fn_x4
ALU = mybir.AluOpType
COPY = mybir.ActivationFunctionType.Copy

P = 128
PACK = 4
PASSES = K // (P * PACK)
HALF = 128
HALVES = J // HALF
BUNDLE = 8
GH = HALF // BUNDLE


def tile_list_headpicks_levelled_timeslook_pl_kernel(
    tc, xt_words, xt_scales, w_words, w_scales, wb_words, wb_scales, tz, offs, offs2, out_0, out_1, out_2
):
    nc = tc.nc
    with ExitStack() as ctx:
        keep = ctx.enter_context(tc.tile_pool(name="keep", bufs=1))
        psum = ctx.enter_context(tc.psum_pool(name="psum", bufs=1))

        lists = keep.tile([P, J // 16], U16, name="lists")
        lists2 = keep.tile([P, J // 16], U16, name="lists2")
        xs_win = keep.tile([P, T], U8, name="xs_win", tag="xs_win", align_bytes=64)
        ws_raw = keep.tile([P, R], U8, name="ws_raw", tag="ws_raw", align_bytes=64)
        plane = keep.tile([P, PASSES, J + R], U8, name="plane", align_bytes=64)
        wbs = keep.tile([P, N], U8, name="wbs", align_bytes=64)
        nc.vector.memset(xs_win[:].bitcast(I32), 0)
        nc.vector.memset(ws_raw[:].bitcast(I32), 0)
        nc.gpsimd.memset(plane[:].rearrange("p s c -> p (s c)").bitcast(I32), 0)
        nc.gpsimd.memset(wbs[:].bitcast(I32), 0)

        nc.sync.dma_start(lists[:], offs)
        nc.sync.dma_start(lists2[:], offs2)
        nc.sync.dma_start(xs_win[0:P:4, :].bitcast(I32), xt_scales.bitcast(I32).rearrange("z q c -> q z c"))
        nc.sync.dma_start(ws_raw[0:P:4, :].bitcast(I32), w_scales.bitcast(I32).rearrange("z q c -> q z c"))
        nc.sync.dma_start(ws_raw[2:P:8, :].bitcast(I32), wb_scales[0].bitcast(I32))
        xw_win = [keep.tile([P, T], I32, name="xw_win%d" % z, align_bytes=64) for z in range(PASSES)]
        for z in range(PASSES):
            nc.sync.dma_start(xw_win[z][:], xt_words[z].rearrange("p c r -> p (c r)").bitcast(I32))
        ww_raw = keep.tile([P, PASSES, R // 2], I32, name="ww_raw", tag="ww_raw", align_bytes=64)
        nc.sync.dma_start(ww_raw[:], w_words.bitcast(I32).rearrange("z p c -> p z c"))
        wbw_raw = keep.tile([P, N], I32, name="wbw_raw", align_bytes=64)
        nc.sync.dma_start(wbw_raw[:], wb_words[0].rearrange("p c r -> p (c r)").bitcast(I32))
        tz_rows = tz.rearrange("(p t) z -> p t z", t=PACK)
        tz_first = keep.tile([P, 1, Z], F32, name="tz_first", align_bytes=64)
        nc.sync.dma_start(tz_first[:], tz_rows[:, 0:1, :])

        xs_got = keep.tile([P, J], U8, name="xs_got", tag="xs_got", align_bytes=64)
        nc.vector.tensor_copy(xs_got[:], xs_win[:].indirect(lists[:]))
        staged = keep.tile([P, J + R], U8, name="staged", align_bytes=64)
        nc.vector.tensor_copy(
            staged[:, J:].rearrange("p (t c i) -> p c t i", t=PACK, i=16),
            ws_raw[:].rearrange("p (c i t) -> p c t i", t=PACK, i=16),
        )
        nc.vector.tensor_copy(staged[:, :J].bitcast(I32), xs_got[:].bitcast(I32))
        for x in range(4):
            (nc.sync, nc.scalar)[x % 2].dma_start(
                plane[32 * x : 32 * x + 4].rearrange("p s c -> p (s c)").bitcast(I32),
                staged[32 * x : 32 * x + 32 : 4, :].bitcast(I32),
            )
        tz_rest = keep.tile([P, PACK - 1, Z], F32, name="tz_rest", tag="xs_got", align_bytes=64)
        nc.sync.dma_start(tz_rest[:], tz_rows[:, 1:PACK, :])
        for x in range(4):
            nc.sync.dma_start(
                wbs[32 * x : 32 * x + 4, :].bitcast(I32), staged[32 * x + 2 : 32 * x + 32 : 8, J:].bitcast(I32)
            )
        tz_win = [tz_first[:, 0, :]] + [tz_rest[:, t, :] for t in range(PACK - 1)]

        xw_got = [
            keep.tile([P, J], U32, name="xw_got%d" % z, tag=("xs_win", "ws_raw")[z], align_bytes=64)
            for z in range(PASSES)
        ]
        for z in range(PASSES):
            nc.vector.tensor_copy(xw_got[z][:], xw_win[z][:].bitcast(U32).indirect(lists[:]))
        ww = keep.tile([P, PASSES, 2 * R], U8, name="ww", align_bytes=64)
        for z in range(PASSES):
            nc.vector.tensor_copy(
                ww[:, z, :].bitcast(U16).rearrange("p (t c i) -> p c t i", t=PACK, i=8),
                ww_raw[:, z, :].bitcast(U16).rearrange("p (c i t) -> p c t i", t=PACK, i=8),
            )
        wbw = keep.tile([P, N], I32, name="wbw", tag="ww_raw", align_bytes=64)
        nc.vector.tensor_copy(
            wbw[:].rearrange("p (t c i) -> p c t i", t=PACK, i=4),
            wbw_raw[:].rearrange("p (c i t) -> p c t i", t=PACK, i=4),
        )

        a_ps = [psum.tile([P, PACK, HALF], F32, name="a_ps%d" % h) for h in range(HALVES)]
        for h in range(HALVES):
            cols = slice(h * HALF, (h + 1) * HALF)
            for t in range(PACK):
                for z in range(PASSES):
                    nc.tensor.matmul_mx(
                        out=a_ps[h][:, t, :],
                        lhsT=ww[:, z, 2 * P * t : 2 * P * (t + 1)].bitcast(E2M1),
                        lhsT_scale=plane[:, z, J + P * t : J + P * (t + 1)],
                        rhs=xw_got[z][:, cols].bitcast(E4M3),
                        rhs_scale=plane[:, z, cols],
                        start=(z == 0),
                        stop=(z == PASSES - 1),
                    )

        tz_got = keep.tile([P, PACK, J], F32, name="tz_got", align_bytes=64)
        for t in range(PACK):
            nc.scalar.activation(tz_got[:, t, :], tz_win[t].indirect(lists2[:]), COPY)

        out_rows = out_0.rearrange("(p t) j -> p t j", t=PACK)
        out_words = out_1[0].rearrange("p c r -> p (c r)").bitcast(I32)
        y_words = keep.tile([P, J], I32, name="y_words", align_bytes=64)
        y_scales = keep.tile([P, J], U8, name="y_scales", align_bytes=64)
        p_ps = [psum.tile([P, PACK, HALF], F32, name="p_ps%d" % h) for h in range(HALVES)]
        for h in range(HALVES):
            sums = keep.tile([P, GH, PACK], F32, name="sums%d" % h, tag="sums", align_bytes=64)
            by_bundle = a_ps[h][:].rearrange("p t (g e) -> p g t e", e=BUNDLE)
            nc.vector.tensor_reduce(sums[:], by_bundle, mybir.AxisListType.X, ALU.add)
            hid = keep.tile([P, BUNDLE, GH, PACK], BF16, name="hid%d" % h, tag="hid%d" % h, align_bytes=64)
            for e in range(BUNDLE):
                nc.vector.scalar_tensor_tensor(
                    hid[:, e], sums[:], -1.0 / BUNDLE, by_bundle[:, :, :, e], ALU.mult, ALU.add
                )
            hid_words = keep.tile([P, HALF], U32, name="hid_words%d" % h, align_bytes=64)
            hid_scales = keep.tile([P, HALF], U8, name="hid_scales%d" % h, align_bytes=64)
            nc.vector.quantize_mx(
                out=hid_words[:].bitcast(E5M2), scales=hid_scales[:], in_=hid[:].rearrange("p e g t -> p (e g t)")
            )
            for t in range(PACK):
                nc.tensor.matmul_mx(
                    out=p_ps[h][:, t, :],
                    lhsT=wbw[:, P * t : P * (t + 1)].bitcast(E5M2),
                    lhsT_scale=wbs[:, P * t : P * (t + 1)],
                    rhs=hid_words[:].bitcast(E5M2),
                    rhs_scale=hid_scales[:],
                    start=True,
                    stop=True,
                )
        for h in range(HALVES):
            cols = slice(h * HALF, (h + 1) * HALF)
            y = keep.tile([P, PACK, HALF], F32, name="y%d" % h, tag=("hid1", "y1")[h], align_bytes=64)
            nc.vector.tensor_tensor(
                y[:].rearrange("p t (g e) -> p t g e", e=BUNDLE),
                p_ps[h][:].rearrange("p t (e g) -> p t g e", e=BUNDLE),
                tz_got[:, :, cols].rearrange("p t (g e) -> p t g e", e=BUNDLE),
                ALU.mult,
            )
            nc.sync.dma_start(out_rows[:, :, cols], y[:])
            y_bf = keep.tile([P, HALF, PACK], BF16, name="y_bf%d" % h, align_bytes=64)
            dst = y_bf[:].rearrange("p (c i) t -> p c t i", i=4)
            src = y[:].rearrange("p t (c i) -> p c t i", i=4)
            if h == 0:
                nc.scalar.copy(dst, src)
            else:
                nc.vector.tensor_copy(dst, src)
            nc.vector.quantize_mx(
                out=y_words[:, cols].bitcast(E4M3), scales=y_scales[:, cols], in_=y_bf[:].rearrange("p j t -> p (j t)")
            )
            nc.sync.dma_start(out_words[:, cols], y_words[:, cols])
        for x in range(4):
            eng = nc.scalar if x % 2 == 0 else nc.sync
            eng.dma_start(out_2[0, 4 * x : 4 * x + 4, :].bitcast(I32), y_scales[32 * x : 32 * x + 4, :].bitcast(I32))
